import numpy as np
import ml_dtypes


def mxq(x, axis, fmt="e4m3"):
    dtype, down = {"e4m3": (ml_dtypes.float8_e4m3fn, 7), "e5m2": (ml_dtypes.float8_e5m2, 14)}[fmt]
    v = np.moveaxis(np.asarray(x, np.float32).astype(ml_dtypes.bfloat16).astype(np.float64), axis, -1)
    blocks = v.reshape(v.shape[:-1] + (-1, 32))
    amax = np.abs(blocks).max(-1, keepdims=True)
    byte = np.maximum(np.where(amax > 0, np.frexp(amax)[1] - 1 + 127, 0) - down, 1)
    scale = np.exp2(byte - 127.0)
    codes = (blocks / scale).astype(np.float32).astype(dtype).astype(np.float64)
    return np.moveaxis((codes * scale).reshape(v.shape), -1, axis)


WIDE = False


def mx_kscale(k):
    if not WIDE:
        return np.ones(k)
    levels = np.array([10, -10, 5, -5, 0])
    if k % 512:
        return np.exp2(np.random.permutation(np.resize(levels, k // 32))).repeat(32)
    a = np.empty((k // 512, 16))
    for p in range(k // 512):
        a[p, :8] = np.random.permutation(np.resize(levels, 8))
        for g in range(8):
            far = levels[np.abs(levels - a[p, g]) >= 10]
            a[p, g + 8] = far[np.random.randint(len(far))]
    return np.exp2(a.ravel()).repeat(32)


def f64(x):
    return np.asarray(x).astype(np.float64)


def striped(idx):
    return np.tile(np.asarray(idx).reshape(-1, 16).T, (8, 1)).astype(np.uint16)


def unstriped(offs):
    return offs[:16].T.reshape(-1).astype(np.int64)


E2M1 = np.array([0.0, 0.5, 1.0, 1.5, 2.0, 3.0, 4.0, 6.0, -0.0, -0.5, -1.0, -1.5, -2.0, -3.0, -4.0, -6.0])


def pack_weight(w, fmt):
    k, n = w.shape
    w = f64(np.asarray(w, np.float32).astype(ml_dtypes.bfloat16)).reshape(k // 32, 32, n)
    amax = np.abs(w).max(1)
    if fmt == "e4m3":
        byte = np.frexp(amax)[1] - 1 + 127 - 7
    else:
        mant, ex = np.frexp(amax / 6.0)
        byte = np.where(mant > 0.5, ex, ex - 1) + 127
    byte = np.clip(np.where(amax > 0, byte, 1), 1, 254)
    scaled = (w * np.exp2(127.0 - byte)[:, None, :]).reshape(k, n).astype(np.float32)
    by_word = np.ascontiguousarray(scaled.reshape(k // 512, 128, 4, n).transpose(0, 1, 3, 2))
    if fmt == "e4m3":
        words = by_word.astype(ml_dtypes.float8_e4m3fn).view(np.uint8)
    else:
        c = by_word.astype(ml_dtypes.float4_e2m1fn).view(np.uint8) & 0xF
        words = (c[..., 0::2] | (c[..., 1::2] << 4)).reshape(k // 512, 128, 2 * n)
    return np.ascontiguousarray(words), np.ascontiguousarray(byte.astype(np.uint8).reshape(k // 512, 16, n))


def unpack_weight(words, scales, fmt):
    g, _, n = scales.shape
    words = np.ascontiguousarray(words).reshape(g, 128, n, -1)
    if fmt == "e4m3":
        vals = words.view(ml_dtypes.float8_e4m3fn).astype(np.float64)
    else:
        nib = np.empty((g, 128, n, 4), np.uint8)
        nib[..., 0::2] = words & 0xF
        nib[..., 1::2] = words >> 4
        vals = E2M1[nib]
    vals = vals * np.repeat(np.exp2(scales.astype(np.float64) - 127.0), 8, axis=1)[..., None]
    return vals.transpose(0, 1, 3, 2).reshape(g * 512, n)


D, E, T, I, Q = 512, 512, 2048, 512, 128


def setup_inputs():
    n = np.random.standard_normal
    idx4 = np.random.permutation(I)[:I]
    idx = np.random.permutation(T)[:I]
    fd = mx_kscale(D)
    fe = mx_kscale(E)
    keysp = pack_weight(n((D, T)) / fd[:, None], "e4m3")
    valsp = pack_weight(n((E, T)) / fe[:, None], "e4m3")
    return {
        "query": (n((D, Q)) * 0.8 / np.sqrt(D) * fd[:, None]).astype(np.float32),
        "keys_words": keysp[0],
        "keys_scales": keysp[1],
        "reserve": (np.random.uniform(0.2, 1.0, (Q, 1))).astype(np.float32),
        "gout": (n((E, Q)) * 1 / np.sqrt(E) * fe[:, None]).astype(np.float32),
        "vals_words": valsp[0],
        "vals_scales": valsp[1],
        "dquery": (n((D, Q)) * 1.0 / np.sqrt(D) * fd[:, None]).astype(np.float32),
        "base": (0.5 * n((Q, T))).astype(np.float32),
        "offs4": striped(idx4),
        "offs": striped(idx),
    }


def reference(query, keys_words, keys_scales, reserve, gout, vals_words, vals_scales, dquery, base, offs4, offs):
    idx4 = unstriped(offs4)
    idx = unstriped(offs)
    keysu = unpack_weight(keys_words, keys_scales, "e4m3")
    valsu = unpack_weight(vals_words, vals_scales, "e4m3")
    queryq = mxq(f64(query), 0, "e4m3")
    keysidxg = keysu[:, idx]
    a = queryq.T @ keysidxg
    dqueryq = mxq(f64(dquery), 0, "e4m3")
    ta = dqueryq.T @ keysidxg
    p = np.exp(a - np.max(a, axis=1, keepdims=True))
    r = p / np.sum(p, axis=1, keepdims=True)
    u0 = np.sqrt(r * r[:, idx4])
    goutq = mxq(f64(gout), 0, "e4m3")
    valsidxg = valsu[:, idx]
    c0 = goutq.T @ valsidxg
    du0 = c0 / (np.sum(u0, axis=1, keepdims=True) + f64(reserve)) + np.sum(c0 * u0 / np.square(np.sum(u0, axis=1, keepdims=True) + f64(reserve)) * (-1.0), axis=1, keepdims=True)
    e1 = du0 * 0.5 / np.sqrt(r * r[:, idx4]) * r
    s1 = np.zeros((Q, I))
    s1[:, idx4] = e1
    dr = du0 * 0.5 / np.sqrt(r * r[:, idx4]) * r[:, idx4] + s1
    dp = dr / np.sum(p, axis=1, keepdims=True) + np.sum(dr * p / np.square(np.sum(p, axis=1, keepdims=True)) * (-1.0), axis=1, keepdims=True)
    tp = ta * p
    tr = (tp - np.sum(tp, axis=1, keepdims=True) * p / np.sum(p, axis=1, keepdims=True)) / np.sum(p, axis=1, keepdims=True)
    tu0 = (tr * r[:, idx4] + tr[:, idx4] * r) * 0.5 / u0
    tdu0 = np.sum(tu0, axis=1, keepdims=True) * c0 / np.square(np.sum(u0, axis=1, keepdims=True) + f64(reserve)) * (-1.0) + np.sum((tu0 * c0 - np.sum(tu0, axis=1, keepdims=True) * (np.sum(u0, axis=1, keepdims=True) + f64(reserve)) * 2.0 * c0 * u0 / np.square(np.sum(u0, axis=1, keepdims=True) + f64(reserve))) / np.square(np.sum(u0, axis=1, keepdims=True) + f64(reserve)) * (-1.0), axis=1, keepdims=True)
    te1 = (tdu0 * 0.5 - (tr * r[:, idx4] + tr[:, idx4] * r) * 0.5 / np.sqrt(r * r[:, idx4]) * du0 * 0.5 / np.sqrt(r * r[:, idx4])) / np.sqrt(r * r[:, idx4]) * r + tr * du0 * 0.5 / np.sqrt(r * r[:, idx4])
    ts1 = np.zeros((Q, I))
    ts1[:, idx4] = te1
    tdr = (tdu0 * 0.5 - (tr * r[:, idx4] + tr[:, idx4] * r) * 0.5 / np.sqrt(r * r[:, idx4]) * du0 * 0.5 / np.sqrt(r * r[:, idx4])) / np.sqrt(r * r[:, idx4]) * r[:, idx4] + tr[:, idx4] * du0 * 0.5 / np.sqrt(r * r[:, idx4]) + ts1
    tdp = (tdr - np.sum(tp, axis=1, keepdims=True) * dr / np.sum(p, axis=1, keepdims=True)) / np.sum(p, axis=1, keepdims=True) + np.sum((tdr * p + tp * dr - np.sum(tp, axis=1, keepdims=True) * np.sum(p, axis=1, keepdims=True) * 2.0 * dr * p / np.square(np.sum(p, axis=1, keepdims=True))) / np.square(np.sum(p, axis=1, keepdims=True)) * (-1.0), axis=1, keepdims=True)
    tda = tdp * p + tp * dp
    gs = tda * 512.0
    gf = np.zeros((Q, T))
    gf[:, idx] = gs
    y = f64(base) + gf
    return y

@@ -1,0 +1,230 @@
+from contextlib import ExitStack
+
+import concourse.mybir as mybir
+
+F32 = mybir.dt.float32
+BF16 = mybir.dt.bfloat16
+I32 = mybir.dt.int32
+U32 = mybir.dt.uint32
+U16 = mybir.dt.uint16
+U8 = mybir.dt.uint8
+FP8X4 = mybir.dt.float8_e4m3fn_x4
+ALU = mybir.AluOpType
+ACT = mybir.ActivationFunctionType
+AXIS = mybir.AxisListType
+
+P = 128
+K = 512
+TOKENS = 2048
+SLOTS = 512
+ROWS = 128
+PACK = 4
+SPARE = 16
+LIST_ROWS = 16
+VECTOR_SHARE = 160
+STORE_WIDTHS = (512, 512, 512, 512)
+FLOOR = 2.0**-100
+
+FLOPS = 3 * 2 * K * ROWS * SLOTS
+
+
+def tile_attend_hvdirect_agreed_s_kernel(
+    tc, query, keys_words, keys_scales, reserve, gout, vals_words, vals_scales, dquery, base, offs4, offs, out
+):
+    nc = tc.nc
+    with ExitStack() as ctx:
+        lists = ctx.enter_context(tc.tile_pool(name="lists", bufs=1))
+        sb = ctx.enter_context(tc.tile_pool(name="sb", bufs=1))
+        psum = ctx.enter_context(tc.psum_pool(name="psum", bufs=1))
+
+        def wide(name, columns=SLOTS):
+            return sb.tile([P, columns], F32, name=name)
+
+        def column(name):
+            return sb.tile([P, 1], F32, name=name)
+
+        def load_words(name, words, tag):
+            pool_words = sb.tile([P, TOKENS], I32, name=name, tag=tag)
+            nc.sync.dma_start(out=pool_words[:], in_=words[0].rearrange("p n t -> p (n t)").bitcast(I32))
+            return pool_words
+
+        def load_scales(name, scales, tag, clearer, queue):
+            pool_scales = sb.tile([P, TOKENS], U8, name=name, tag=tag)
+            clearer.memset(pool_scales[:].bitcast(I32), 0)
+            for quadrant in range(4):
+                queue.dma_start(
+                    out=pool_scales[32 * quadrant : 32 * quadrant + 4, :].bitcast(I32),
+                    in_=scales[0, 4 * quadrant : 4 * quadrant + 4, :].bitcast(I32),
+                )
+            return pool_scales
+
+        def load_rows(name, rows, tag):
+            raw = sb.tile([P, PACK, ROWS], F32, name=name, tag=tag)
+            nc.sync.dma_start(out=raw[:], in_=rows.rearrange("(p j) w -> p j w", j=PACK))
+            return raw
+
+        def gather_words(name, pool_words):
+            listed = sb.tile([P, SLOTS], U32, name=name, align_bytes=64)
+            nc.vector.tensor_copy(listed[:], pool_words[:].bitcast(U32).indirect(token_list[:]))
+            return listed
+
+        def gather_scales(name, pool_scales):
+            listed = sb.tile([P, SLOTS], U8, name=name, align_bytes=64)
+            nc.vector.tensor_copy(listed[:], pool_scales[:].indirect(token_list[:]))
+            return listed
+
+        def round_rows(name, raw):
+            grouped = sb.tile([P, ROWS, PACK], BF16, name=name, align_bytes=64)
+            nc.scalar.copy(out=grouped[:], in_=raw[:].rearrange("p j w -> p w j"))
+            return grouped
+
+        def quantise(name, grouped):
+            codes = sb.tile([P, ROWS], U32, name=name + "_codes", align_bytes=64)
+            scales = sb.tile([P, ROWS], U8, name=name + "_scales", align_bytes=64)
+            nc.vector.quantize_mx(
+                out=codes[:].bitcast(FP8X4), scales=scales[:], in_=grouped[:].rearrange("p w j -> p (w j)")
+            )
+            return codes, scales
+
+        def product(name, rows_mx, listed_words, listed_scales):
+            bank = psum.tile([P, SLOTS], F32, name=name)
+            nc.tensor.matmul_mx(
+                out=bank[:],
+                lhsT=rows_mx[0][:].bitcast(FP8X4),
+                lhsT_scale=rows_mx[1][:],
+                rhs=listed_words[:].bitcast(FP8X4),
+                rhs_scale=listed_scales[:],
+                start=True,
+                stop=True,
+            )
+            return bank
+
+        token_list = lists.tile([P, SLOTS // LIST_ROWS], U16, name="token_list")
+        partner_list = lists.tile([P, SLOTS // LIST_ROWS], U16, name="partner_list")
+        nc.sync.dma_start(token_list[:], offs)
+        key_scales = load_scales("key_scales", keys_scales, "first", nc.vector, nc.scalar)
+        query_raw = load_rows("query_raw", query, "query_then_values")
+        key_words = load_words("key_words", keys_words, "second")
+        value_scales = load_scales("value_scales", vals_scales, "value_scales", nc.gpsimd, nc.gpsimd)
+        dquery_raw = load_rows("dquery_raw", dquery, "dquery")
+        nc.sync.dma_start(partner_list[:], offs4)
+        res = column("res")
+        nc.gpsimd.dma_start(out=res[:], in_=reserve)
+
+        r = wide("r", SLOTS + SPARE)
+        tr = wide("tr", SLOTS + SPARE)
+        placed = wide("placed", TOKENS)
+        back_v = wide("back_v")
+        back_s = wide("back_s")
+        floor = column("floor")
+        nc.vector.memset(r[:, SLOTS:], 0.0)
+        nc.vector.memset(tr[:, SLOTS:], 0.0)
+        nc.vector.memset(floor[:], FLOOR)
+        nc.vector.memset(placed[:], 0.0)
+        nc.vector.memset(back_v[:], 0.0)
+        nc.vector.memset(back_s[:], 0.0)
+
+        listed_key_scales = gather_scales("listed_key_scales", key_scales)
+        query_mx = quantise("query", round_rows("query_bf", query_raw))
+        value_words = load_words("value_words", vals_words, "query_then_values")
+        gout_raw = load_rows("gout_raw", gout, "first")
+        listed_keys = gather_words("listed_keys", key_words)
+        result = sb.tile([P, TOKENS], F32, name="result", tag="second")
+        nc.sync.dma_start(out=result[:], in_=base)
+        a = product("a", query_mx, listed_keys, listed_key_scales)
+        listed_value_scales = gather_scales("listed_value_scales", value_scales)
+        dquery_mx = quantise("dquery", round_rows("dquery_bf", dquery_raw))
+        ta = product("ta", dquery_mx, listed_keys, listed_key_scales)
+        gout_bf = round_rows("gout_bf", gout_raw)
+
+        res2 = column("res2")
+        nc.vector.tensor_scalar(res2[:], res[:], 2.0, None, ALU.mult)
+        neg_max = column("neg_max")
+        nc.vector.tensor_reduce(neg_max[:], a[:], AXIS.X, ALU.max, negate=True)
+        p = wide("p")
+        p_sum = column("p_sum")
+        nc.scalar.activation(p[:], a[:], ACT.Exp, bias=neg_max[:], accum_out=p_sum[:])
+
+        listed_values = gather_words("listed_values", value_words)
+        gout_mx = quantise("gout", gout_bf)
+        c = product("c", gout_mx, listed_values, listed_value_scales)
+
+        inv_p_sum = column("inv_p_sum")
+        nc.vector.reciprocal(inv_p_sum[:], p_sum[:])
+        nc.scalar.activation(r[:, :SLOTS], p[:], ACT.Copy, scale=inv_p_sum[:])
+        tp = wide("tp")
+        tp_sum = column("tp_sum")
+        nc.vector.scalar_tensor_tensor(tp[:], ta[:], 1.0, p[:], ALU.mult, ALU.mult, accum_out=tp_sum[:])
+        rr = wide("rr")
+        nc.vector.tensor_tensor(rr[:], r[:].indirect(partner_list[:]), p[:], ALU.mult)
+        mean = column("mean")
+        nc.vector.tensor_scalar(mean[:], tp_sum[:], inv_p_sum[:], None, ALU.mult)
+        half_inv_u = wide("half_inv_u")
+        nc.scalar.activation(half_inv_u[:], rr[:], ACT.Abs_reciprocal_sqrt, bias=floor[:], scale=p_sum[:])
+        nc.vector.scalar_tensor_tensor(tr[:, :SLOTS], ta[:], mean[:], r[:, :SLOTS], ALU.subtract, ALU.mult)
+        tr_partner = wide("tr_partner")
+        nc.scalar.activation(tr_partner[:], tr[:].indirect(partner_list[:]), ACT.Copy)
+
+        u = wide("u")
+        u_sum = column("u_sum")
+        nc.vector.scalar_tensor_tensor(u[:], rr[:], 1.0, half_inv_u[:], ALU.mult, ALU.mult, accum_out=u_sum[:])
+        own = wide("own")
+        nc.vector.scalar_tensor_tensor(own[:], ta[:], mean[:], rr[:], ALU.subtract, ALU.mult)
+        z_256th = column("z_256th")
+        nc.vector.tensor_scalar(z_256th[:], u_sum[:], res[:], 1.0 / 128.0, ALU.add, ALU.mult)
+        cu = wide("cu")
+        cu_sum = column("cu_sum")
+        nc.vector.scalar_tensor_tensor(cu[:], c[:], 1.0, u[:], ALU.mult, ALU.mult, accum_out=cu_sum[:])
+        inv_z_256 = column("inv_z_256")
+        nc.vector.reciprocal(inv_z_256[:], z_256th[:])
+        other = wide("other")
+        nc.vector.tensor_tensor(other[:], tr_partner[:], p[:], ALU.mult)
+        gamma = column("gamma")
+        nc.vector.tensor_scalar(gamma[:], cu_sum[:], inv_z_256[:], 1.0 / 128.0, ALU.mult, ALU.mult)
+        trr = wide("trr")
+        nc.vector.tensor_tensor(trr[:], own[:], other[:], ALU.add)
+        inv_z = column("inv_z")
+        nc.vector.tensor_scalar(inv_z[:], inv_z_256[:], 1.0 / 128.0, None, ALU.mult)
+        tu = wide("tu")
+        tu_sum = column("tu_sum")
+        nc.vector.scalar_tensor_tensor(
+            tu[:], trr[:], inv_z_256[:], half_inv_u[:], ALU.mult, ALU.mult, accum_out=tu_sum[:]
+        )
+        half_d = column("half_d")
+        nc.vector.tensor_scalar(half_d[:], gamma[:], res2[:], inv_z_256[:], ALU.mult, ALU.mult)
+        tr_term = wide("tr_term")
+        nc.scalar.activation(tr_term[:], tr[:, :SLOTS], ACT.Copy, scale=half_d[:])
+        kappa = column("kappa")
+        nc.vector.tensor_scalar(kappa[:], tu_sum[:], inv_z[:], None, ALU.mult)
+        neg_v = wide("neg_v")
+        nc.vector.scalar_tensor_tensor(neg_v[:], u[:], kappa[:], tu[:], ALU.mult, ALU.subtract)
+        shift = column("shift")
+        nc.vector.tensor_scalar(shift[:], kappa[:], gamma[:], res[:], ALU.mult, ALU.mult)
+        neg_x = wide("neg_x")
+        neg_x_sum = column("neg_x_sum")
+        nc.vector.scalar_tensor_tensor(
+            neg_x[:], c[:], gamma[:], neg_v[:], ALU.subtract, ALU.mult, accum_out=neg_x_sum[:]
+        )
+        neg_nu = column("neg_nu")
+        nc.vector.tensor_scalar(neg_nu[:], neg_x_sum[:], shift[:], inv_z[:], ALU.subtract, ALU.mult)
+        g = wide("g")
+        g_sum = column("g_sum")
+        nc.vector.scalar_tensor_tensor(g[:], u[:], neg_nu[:], neg_x[:], ALU.mult, ALU.subtract, accum_out=g_sum[:])
+
+        cut = VECTOR_SHARE // LIST_ROWS
+        nc.scalar.activation(back_s[:].indirect(partner_list[:, cut:]), g[:, VECTOR_SHARE:], ACT.Copy)
+        nc.vector.tensor_copy(back_v[:].indirect(partner_list[:, :cut]), g[:, :VECTOR_SHARE])
+        softmax_term = wide("softmax_term")
+        nc.vector.scalar_tensor_tensor(softmax_term[:], r[:, :SLOTS], g_sum[:], tr_term[:], ALU.mult, ALU.add)
+        direct = wide("direct")
+        nc.vector.scalar_tensor_tensor(direct[:], softmax_term[:], -2.0, g[:], ALU.mult, ALU.add)
+        partial = wide("partial")
+        nc.vector.tensor_tensor(partial[:], direct[:], back_v[:], ALU.add)
+        nc.vector.tensor_tensor(placed[:].indirect(token_list[:]), partial[:], back_s[:], ALU.add)
+
+        first = 0
+        for width in STORE_WIDTHS:
+            cols = slice(first, first + width)
+            nc.vector.tensor_tensor(result[:, cols], result[:, cols], placed[:, cols], ALU.add)
+            nc.sync.dma_start(out=out[:, cols], in_=result[:, cols])
+            first += width

@@ -21,8 +21,9 @@ ROWS = 128
 PACK = 4
 SPARE = 16
 LIST_ROWS = 16
-VECTOR_SHARE = 160
-STORE_WIDTHS = (512, 512, 512, 512)
+VECTOR_SHARE = 96
+SCALAR_SHARES = (224, 192)
+STORE_WIDTHS = (256, 512, 512, 512, 256)
 FLOOR = 2.0**-100
 
 FLOPS = 3 * 2 * K * ROWS * SLOTS
@@ -37,61 +38,63 @@ def tile_attend_hvdirect_agreed_s_kernel(
         sb = ctx.enter_context(tc.tile_pool(name="sb", bufs=1))
         psum = ctx.enter_context(tc.psum_pool(name="psum", bufs=1))
 
-        def wide(name, columns=SLOTS):
-            return sb.tile([P, columns], F32, name=name)
+        def wide(name, columns=SLOTS, tag=None):
+            return sb.tile([P, columns], F32, name=name, tag=tag or name, align_bytes=64)
 
-        def column(name):
-            return sb.tile([P, 1], F32, name=name)
+        def column(name, tag=None):
+            return sb.tile([P, 1], F32, name=name, tag=tag or name, align_bytes=64)
 
-        def load_words(name, words, tag):
-            pool_words = sb.tile([P, TOKENS], I32, name=name, tag=tag)
+        def load_words(name, words):
+            pool_words = sb.tile([P, TOKENS], I32, name=name, tag=name, align_bytes=64)
             nc.sync.dma_start(out=pool_words[:], in_=words[0].rearrange("p n t -> p (n t)").bitcast(I32))
             return pool_words
 
-        def load_scales(name, scales, tag, clearer, queue):
-            pool_scales = sb.tile([P, TOKENS], U8, name=name, tag=tag)
-            clearer.memset(pool_scales[:].bitcast(I32), 0)
-            for quadrant in range(4):
+        def load_scales(name, scales, queues):
+            pool_scales = sb.tile([P, TOKENS], U8, name=name)
+            nc.vector.memset(pool_scales[:].bitcast(I32), 0)
+            for quadrant, queue in enumerate(queues):
                 queue.dma_start(
                     out=pool_scales[32 * quadrant : 32 * quadrant + 4, :].bitcast(I32),
                     in_=scales[0, 4 * quadrant : 4 * quadrant + 4, :].bitcast(I32),
                 )
             return pool_scales
 
-        def load_rows(name, rows, tag):
-            raw = sb.tile([P, PACK, ROWS], F32, name=name, tag=tag)
+        def load_rows(name, rows):
+            raw = sb.tile([P, PACK, ROWS], F32, name=name)
             nc.sync.dma_start(out=raw[:], in_=rows.rearrange("(p j) w -> p j w", j=PACK))
             return raw
 
         def gather_words(name, pool_words):
-            listed = sb.tile([P, SLOTS], U32, name=name, align_bytes=64)
+            listed = sb.tile([P, SLOTS], U32, name=name, tag=name, align_bytes=64)
             nc.vector.tensor_copy(listed[:], pool_words[:].bitcast(U32).indirect(token_list[:]))
             return listed
 
-        def gather_scales(name, pool_scales):
-            listed = sb.tile([P, SLOTS], U8, name=name, align_bytes=64)
+        def gather_scales(name, pool_scales, tag):
+            listed = sb.tile([P, SLOTS], U8, name=name, tag=tag, align_bytes=64)
             nc.vector.tensor_copy(listed[:], pool_scales[:].indirect(token_list[:]))
             return listed
 
-        def round_rows(name, raw):
-            grouped = sb.tile([P, ROWS, PACK], BF16, name=name, align_bytes=64)
-            nc.scalar.copy(out=grouped[:], in_=raw[:].rearrange("p j w -> p w j"))
+        def round_rows(name, raws, copy):
+            grouped = sb.tile([P, len(raws) * ROWS, PACK], BF16, name=name, align_bytes=64)
+            for place, raw in enumerate(raws):
+                copy(out=grouped[:, place * ROWS : (place + 1) * ROWS, :], in_=raw[:].rearrange("p j w -> p w j"))
             return grouped
 
         def quantise(name, grouped):
-            codes = sb.tile([P, ROWS], U32, name=name + "_codes", align_bytes=64)
-            scales = sb.tile([P, ROWS], U8, name=name + "_scales", align_bytes=64)
+            codes = sb.tile([P, grouped.shape[1]], U32, name=name + "_codes", align_bytes=64)
+            scales = sb.tile([P, grouped.shape[1]], U8, name=name + "_scales", align_bytes=64)
             nc.vector.quantize_mx(
                 out=codes[:].bitcast(FP8X4), scales=scales[:], in_=grouped[:].rearrange("p w j -> p (w j)")
             )
             return codes, scales
 
-        def product(name, rows_mx, listed_words, listed_scales):
+        def product(name, rows_mx, place, listed_words, listed_scales):
+            rows = slice(place * ROWS, (place + 1) * ROWS)
             bank = psum.tile([P, SLOTS], F32, name=name)
             nc.tensor.matmul_mx(
                 out=bank[:],
-                lhsT=rows_mx[0][:].bitcast(FP8X4),
-                lhsT_scale=rows_mx[1][:],
+                lhsT=rows_mx[0][:, rows].bitcast(FP8X4),
+                lhsT_scale=rows_mx[1][:, rows],
                 rhs=listed_words[:].bitcast(FP8X4),
                 rhs_scale=listed_scales[:],
                 start=True,
@@ -102,40 +105,32 @@ def tile_attend_hvdirect_agreed_s_kernel(
         token_list = lists.tile([P, SLOTS // LIST_ROWS], U16, name="token_list")
         partner_list = lists.tile([P, SLOTS // LIST_ROWS], U16, name="partner_list")
         nc.sync.dma_start(token_list[:], offs)
-        key_scales = load_scales("key_scales", keys_scales, "first", nc.vector, nc.scalar)
-        query_raw = load_rows("query_raw", query, "query_then_values")
-        key_words = load_words("key_words", keys_words, "second")
-        value_scales = load_scales("value_scales", vals_scales, "value_scales", nc.gpsimd, nc.gpsimd)
-        dquery_raw = load_rows("dquery_raw", dquery, "dquery")
+        query_raw = load_rows("query_raw", query)
+        key_scales = load_scales("key_scales", keys_scales, (nc.sync, nc.sync, nc.scalar, nc.scalar))
+        key_words = load_words("key_words", keys_words)
+        value_scales = load_scales("value_scales", vals_scales, (nc.scalar,) * 4)
+        dquery_raw = load_rows("dquery_raw", dquery)
+        gout_raw = load_rows("gout_raw", gout)
+        value_words = load_words("value_words", vals_words)
         nc.sync.dma_start(partner_list[:], offs4)
         res = column("res")
-        nc.gpsimd.dma_start(out=res[:], in_=reserve)
+        nc.sync.dma_start(out=res[:], in_=reserve)
+        result = wide("result", TOKENS)
+        nc.sync.dma_start(out=result[:], in_=base)
 
         r = wide("r", SLOTS + SPARE)
         tr = wide("tr", SLOTS + SPARE)
-        placed = wide("placed", TOKENS)
-        back_v = wide("back_v")
-        back_s = wide("back_s")
         floor = column("floor")
         nc.vector.memset(r[:, SLOTS:], 0.0)
         nc.vector.memset(tr[:, SLOTS:], 0.0)
         nc.vector.memset(floor[:], FLOOR)
-        nc.vector.memset(placed[:], 0.0)
-        nc.vector.memset(back_v[:], 0.0)
-        nc.vector.memset(back_s[:], 0.0)
 
-        listed_key_scales = gather_scales("listed_key_scales", key_scales)
-        query_mx = quantise("query", round_rows("query_bf", query_raw))
-        value_words = load_words("value_words", vals_words, "query_then_values")
-        gout_raw = load_rows("gout_raw", gout, "first")
+        listed_key_scales = gather_scales("listed_key_scales", key_scales, "listed_key_scales")
+        query_mx = quantise("query", round_rows("query_bf", [query_raw], nc.vector.tensor_copy))
         listed_keys = gather_words("listed_keys", key_words)
-        result = sb.tile([P, TOKENS], F32, name="result", tag="second")
-        nc.sync.dma_start(out=result[:], in_=base)
-        a = product("a", query_mx, listed_keys, listed_key_scales)
-        listed_value_scales = gather_scales("listed_value_scales", value_scales)
-        dquery_mx = quantise("dquery", round_rows("dquery_bf", dquery_raw))
-        ta = product("ta", dquery_mx, listed_keys, listed_key_scales)
-        gout_bf = round_rows("gout_bf", gout_raw)
+        a = product("a", query_mx, 0, listed_keys, listed_key_scales)
+        listed_value_scales = gather_scales("listed_value_scales", value_scales, "key_words")
+        later_bf = round_rows("later_bf", [dquery_raw, gout_raw], nc.scalar.copy)
 
         res2 = column("res2")
         nc.vector.tensor_scalar(res2[:], res[:], 2.0, None, ALU.mult)
@@ -145,31 +140,45 @@ def tile_attend_hvdirect_agreed_s_kernel(
         p_sum = column("p_sum")
         nc.scalar.activation(p[:], a[:], ACT.Exp, bias=neg_max[:], accum_out=p_sum[:])
 
-        listed_values = gather_words("listed_values", value_words)
-        gout_mx = quantise("gout", gout_bf)
-        c = product("c", gout_mx, listed_values, listed_value_scales)
+        scalar_inv_p_sum = column("scalar_inv_p_sum")
+        nc.scalar.activation(scalar_inv_p_sum[:], p_sum[:], ACT.Abs_reciprocal_sqrt, scale=p_sum[:])
 
-        inv_p_sum = column("inv_p_sum")
+        later_mx = quantise("later", later_bf)
+        ta = product("ta", later_mx, 0, listed_keys, listed_key_scales)
+        listed_values = gather_words("listed_values", value_words)
+        c = product("c", later_mx, 1, listed_values, listed_value_scales)
+
+        inv_p_sum = column("inv_p_sum", tag="value_words")
         nc.vector.reciprocal(inv_p_sum[:], p_sum[:])
-        nc.scalar.activation(r[:, :SLOTS], p[:], ACT.Copy, scale=inv_p_sum[:])
         tp = wide("tp")
         tp_sum = column("tp_sum")
         nc.vector.scalar_tensor_tensor(tp[:], ta[:], 1.0, p[:], ALU.mult, ALU.mult, accum_out=tp_sum[:])
-        rr = wide("rr")
-        nc.vector.tensor_tensor(rr[:], r[:].indirect(partner_list[:]), p[:], ALU.mult)
+        nc.gpsimd.tensor_scalar(r[:, :SLOTS], p[:], inv_p_sum[:], 0.0, ALU.mult, ALU.add)
         mean = column("mean")
-        nc.vector.tensor_scalar(mean[:], tp_sum[:], inv_p_sum[:], None, ALU.mult)
-        half_inv_u = wide("half_inv_u")
-        nc.scalar.activation(half_inv_u[:], rr[:], ACT.Abs_reciprocal_sqrt, bias=floor[:], scale=p_sum[:])
+        nc.vector.tensor_scalar(mean[:], tp_sum[:], scalar_inv_p_sum[:], None, ALU.mult)
         nc.vector.scalar_tensor_tensor(tr[:, :SLOTS], ta[:], mean[:], r[:, :SLOTS], ALU.subtract, ALU.mult)
         tr_partner = wide("tr_partner")
         nc.scalar.activation(tr_partner[:], tr[:].indirect(partner_list[:]), ACT.Copy)
+        rr = wide("rr")
+        nc.vector.tensor_tensor(rr[:], r[:].indirect(partner_list[:]), p[:], ALU.mult)
+        half_inv_u = wide("half_inv_u")
+        nc.scalar.activation(half_inv_u[:], rr[:], ACT.Abs_reciprocal_sqrt, bias=floor[:], scale=p_sum[:])
 
+        back_s = wide("back_s", tag="tp")
+        back_v = wide("back_v", tag="listed_keys")
+        placed = wide("placed", TOKENS, tag="value_words")
+        for window in (back_s, back_v, placed):
+            nc.gpsimd.memset(window[:], 0.0)
+
+        own = wide("own")
+        nc.vector.scalar_tensor_tensor(own[:], ta[:], mean[:], rr[:], ALU.subtract, ALU.mult)
+        other = wide("other")
+        nc.vector.tensor_tensor(other[:], tr_partner[:], p[:], ALU.mult)
         u = wide("u")
         u_sum = column("u_sum")
         nc.vector.scalar_tensor_tensor(u[:], rr[:], 1.0, half_inv_u[:], ALU.mult, ALU.mult, accum_out=u_sum[:])
-        own = wide("own")
-        nc.vector.scalar_tensor_tensor(own[:], ta[:], mean[:], rr[:], ALU.subtract, ALU.mult)
+        trr = wide("trr")
+        nc.vector.tensor_tensor(trr[:], own[:], other[:], ALU.add)
         z_256th = column("z_256th")
         nc.vector.tensor_scalar(z_256th[:], u_sum[:], res[:], 1.0 / 128.0, ALU.add, ALU.mult)
         cu = wide("cu")
@@ -177,49 +186,48 @@ def tile_attend_hvdirect_agreed_s_kernel(
         nc.vector.scalar_tensor_tensor(cu[:], c[:], 1.0, u[:], ALU.mult, ALU.mult, accum_out=cu_sum[:])
         inv_z_256 = column("inv_z_256")
         nc.vector.reciprocal(inv_z_256[:], z_256th[:])
-        other = wide("other")
-        nc.vector.tensor_tensor(other[:], tr_partner[:], p[:], ALU.mult)
-        gamma = column("gamma")
-        nc.vector.tensor_scalar(gamma[:], cu_sum[:], inv_z_256[:], 1.0 / 128.0, ALU.mult, ALU.mult)
-        trr = wide("trr")
-        nc.vector.tensor_tensor(trr[:], own[:], other[:], ALU.add)
-        inv_z = column("inv_z")
-        nc.vector.tensor_scalar(inv_z[:], inv_z_256[:], 1.0 / 128.0, None, ALU.mult)
+        neg_inv_z = column("neg_inv_z")
+        nc.vector.tensor_scalar(neg_inv_z[:], inv_z_256[:], -1.0 / 128.0, None, ALU.mult)
         tu = wide("tu")
         tu_sum = column("tu_sum")
         nc.vector.scalar_tensor_tensor(
             tu[:], trr[:], inv_z_256[:], half_inv_u[:], ALU.mult, ALU.mult, accum_out=tu_sum[:]
         )
-        half_d = column("half_d")
-        nc.vector.tensor_scalar(half_d[:], gamma[:], res2[:], inv_z_256[:], ALU.mult, ALU.mult)
+        neg_gamma = column("neg_gamma")
+        nc.vector.tensor_scalar(neg_gamma[:], cu_sum[:], neg_inv_z[:], None, ALU.mult)
+        neg_kappa = column("neg_kappa")
+        nc.vector.tensor_scalar(neg_kappa[:], tu_sum[:], neg_inv_z[:], None, ALU.mult)
+        res_z = column("res_z")
+        nc.scalar.activation(res_z[:], res2[:], ACT.Copy, scale=inv_z_256[:])
+        neg_half_d = column("neg_half_d")
+        nc.scalar.activation(neg_half_d[:], neg_gamma[:], ACT.Copy, scale=res_z[:])
         tr_term = wide("tr_term")
-        nc.scalar.activation(tr_term[:], tr[:, :SLOTS], ACT.Copy, scale=half_d[:])
-        kappa = column("kappa")
-        nc.vector.tensor_scalar(kappa[:], tu_sum[:], inv_z[:], None, ALU.mult)
-        neg_v = wide("neg_v")
-        nc.vector.scalar_tensor_tensor(neg_v[:], u[:], kappa[:], tu[:], ALU.mult, ALU.subtract)
-        shift = column("shift")
-        nc.vector.tensor_scalar(shift[:], kappa[:], gamma[:], res[:], ALU.mult, ALU.mult)
-        neg_x = wide("neg_x")
-        neg_x_sum = column("neg_x_sum")
-        nc.vector.scalar_tensor_tensor(
-            neg_x[:], c[:], gamma[:], neg_v[:], ALU.subtract, ALU.mult, accum_out=neg_x_sum[:]
-        )
-        neg_nu = column("neg_nu")
-        nc.vector.tensor_scalar(neg_nu[:], neg_x_sum[:], shift[:], inv_z[:], ALU.subtract, ALU.mult)
+        nc.scalar.activation(tr_term[:], tr[:, :SLOTS], ACT.Copy, scale=neg_half_d[:])
+        ctu = wide("ctu")
+        ctu_sum = column("ctu_sum")
+        nc.vector.scalar_tensor_tensor(ctu[:], c[:], neg_gamma[:], tu[:], ALU.add, ALU.mult, accum_out=ctu_sum[:])
+        kappa_gamma = column("kappa_gamma")
+        nc.vector.tensor_scalar(kappa_gamma[:], neg_kappa[:], neg_gamma[:], None, ALU.mult)
+        neg_beta = column("neg_beta")
+        nc.vector.tensor_scalar(neg_beta[:], ctu_sum[:], neg_inv_z[:], kappa_gamma[:], ALU.mult, ALU.add)
+        c_terms = wide("c_terms")
+        nc.vector.scalar_tensor_tensor(c_terms[:], cu[:], neg_kappa[:], ctu[:], ALU.mult, ALU.add)
         g = wide("g")
         g_sum = column("g_sum")
-        nc.vector.scalar_tensor_tensor(g[:], u[:], neg_nu[:], neg_x[:], ALU.mult, ALU.subtract, accum_out=g_sum[:])
+        nc.vector.scalar_tensor_tensor(g[:], u[:], neg_beta[:], c_terms[:], ALU.mult, ALU.add, accum_out=g_sum[:])
 
-        cut = VECTOR_SHARE // LIST_ROWS
-        nc.scalar.activation(back_s[:].indirect(partner_list[:, cut:]), g[:, VECTOR_SHARE:], ACT.Copy)
-        nc.vector.tensor_copy(back_v[:].indirect(partner_list[:, :cut]), g[:, :VECTOR_SHARE])
+        first_slot = VECTOR_SHARE
+        for share in SCALAR_SHARES:
+            entries = partner_list[:, first_slot // LIST_ROWS : (first_slot + share) // LIST_ROWS]
+            nc.scalar.activation(back_s[:].indirect(entries), g[:, first_slot : first_slot + share], ACT.Copy)
+            first_slot += share
+        nc.vector.tensor_copy(back_v[:].indirect(partner_list[:, : VECTOR_SHARE // LIST_ROWS]), g[:, :VECTOR_SHARE])
         softmax_term = wide("softmax_term")
-        nc.vector.scalar_tensor_tensor(softmax_term[:], r[:, :SLOTS], g_sum[:], tr_term[:], ALU.mult, ALU.add)
-        direct = wide("direct")
-        nc.vector.scalar_tensor_tensor(direct[:], softmax_term[:], -2.0, g[:], ALU.mult, ALU.add)
+        nc.vector.scalar_tensor_tensor(softmax_term[:], r[:, :SLOTS], g_sum[:], tr_term[:], ALU.mult, ALU.subtract)
+        both = wide("both")
+        nc.vector.tensor_tensor(both[:], g[:], back_v[:], ALU.add)
         partial = wide("partial")
-        nc.vector.tensor_tensor(partial[:], direct[:], back_v[:], ALU.add)
+        nc.vector.scalar_tensor_tensor(partial[:], softmax_term[:], -2.0, both[:], ALU.mult, ALU.add)
         nc.vector.tensor_tensor(placed[:].indirect(token_list[:]), partial[:], back_s[:], ALU.add)
 
         first = 0

@@ -21,8 +21,8 @@ ROWS = 128
 PACK = 4
 SPARE = 16
 LIST_ROWS = 16
-VECTOR_SHARE = 96
-SCALAR_SHARES = (224, 192)
+VECTOR_SHARE = 128
+SCALAR_SHARES = (384,)
 STORE_WIDTHS = (256, 512, 512, 512, 256)
 FLOOR = 2.0**-100
 
@@ -49,12 +49,12 @@ def tile_attend_hvdirect_agreed_s_kernel(
             nc.sync.dma_start(out=pool_words[:], in_=words[0].rearrange("p n t -> p (n t)").bitcast(I32))
             return pool_words
 
-        def load_scales(name, scales, queues):
-            pool_scales = sb.tile([P, TOKENS], U8, name=name)
+        def load_scales(name, scales, first_row, queues):
+            pool_scales = sb.tile([P, TOKENS], U8, name=name, tag=name, align_bytes=64)
             nc.vector.memset(pool_scales[:].bitcast(I32), 0)
             for quadrant, queue in enumerate(queues):
                 queue.dma_start(
-                    out=pool_scales[32 * quadrant : 32 * quadrant + 4, :].bitcast(I32),
+                    out=pool_scales[32 * quadrant + first_row : 32 * quadrant + first_row + 4, :].bitcast(I32),
                     in_=scales[0, 4 * quadrant : 4 * quadrant + 4, :].bitcast(I32),
                 )
             return pool_scales
@@ -96,7 +96,7 @@ def tile_attend_hvdirect_agreed_s_kernel(
                 lhsT=rows_mx[0][:, rows].bitcast(FP8X4),
                 lhsT_scale=rows_mx[1][:, rows],
                 rhs=listed_words[:].bitcast(FP8X4),
-                rhs_scale=listed_scales[:],
+                rhs_scale=listed_scales,
                 start=True,
                 stop=True,
             )
@@ -106,12 +106,12 @@ def tile_attend_hvdirect_agreed_s_kernel(
         partner_list = lists.tile([P, SLOTS // LIST_ROWS], U16, name="partner_list")
         nc.sync.dma_start(token_list[:], offs)
         query_raw = load_rows("query_raw", query)
-        key_scales = load_scales("key_scales", keys_scales, (nc.sync, nc.sync, nc.scalar, nc.scalar))
+        key_scales = load_scales("key_scales", keys_scales, 0, (nc.sync, nc.sync, nc.scalar, nc.scalar))
         key_words = load_words("key_words", keys_words)
-        value_scales = load_scales("value_scales", vals_scales, (nc.scalar,) * 4)
+        value_scales = load_scales("value_scales", vals_scales, 4, (nc.sync,) * 4)
         dquery_raw = load_rows("dquery_raw", dquery)
-        gout_raw = load_rows("gout_raw", gout)
         value_words = load_words("value_words", vals_words)
+        gout_raw = load_rows("gout_raw", gout)
         nc.sync.dma_start(partner_list[:], offs4)
         res = column("res")
         nc.sync.dma_start(out=res[:], in_=reserve)
@@ -124,17 +124,22 @@ def tile_attend_hvdirect_agreed_s_kernel(
         nc.vector.memset(r[:, SLOTS:], 0.0)
         nc.vector.memset(tr[:, SLOTS:], 0.0)
         nc.vector.memset(floor[:], FLOOR)
+        back_s = wide("back_s")
+        back_v = wide("back_v")
+        placed = wide("placed", TOKENS)
+        for window in (back_s, back_v, placed):
+            nc.vector.memset(window[:].bitcast(I32), 0)
 
         listed_key_scales = gather_scales("listed_key_scales", key_scales, "listed_key_scales")
         query_mx = quantise("query", round_rows("query_bf", [query_raw], nc.vector.tensor_copy))
         listed_keys = gather_words("listed_keys", key_words)
-        a = product("a", query_mx, 0, listed_keys, listed_key_scales)
-        listed_value_scales = gather_scales("listed_value_scales", value_scales, "key_words")
-        later_bf = round_rows("later_bf", [dquery_raw, gout_raw], nc.scalar.copy)
+        a = product("a", query_mx, 0, listed_keys, listed_key_scales[:])
+        listed_value_scales = gather_scales("listed_value_scales", value_scales, "listed_value_scales")
+        dquery_bf = round_rows("dquery_bf", [dquery_raw], nc.scalar.copy)
 
         res2 = column("res2")
         nc.vector.tensor_scalar(res2[:], res[:], 2.0, None, ALU.mult)
-        neg_max = column("neg_max")
+        neg_max = column("neg_max", tag="value_scales")
         nc.vector.tensor_reduce(neg_max[:], a[:], AXIS.X, ALU.max, negate=True)
         p = wide("p")
         p_sum = column("p_sum")
@@ -143,17 +148,17 @@ def tile_attend_hvdirect_agreed_s_kernel(
         scalar_inv_p_sum = column("scalar_inv_p_sum")
         nc.scalar.activation(scalar_inv_p_sum[:], p_sum[:], ACT.Abs_reciprocal_sqrt, scale=p_sum[:])
 
-        later_mx = quantise("later", later_bf)
-        ta = product("ta", later_mx, 0, listed_keys, listed_key_scales)
+        ta = product("ta", quantise("dquery", dquery_bf), 0, listed_keys, listed_key_scales[:])
         listed_values = gather_words("listed_values", value_words)
-        c = product("c", later_mx, 1, listed_values, listed_value_scales)
 
         inv_p_sum = column("inv_p_sum", tag="value_words")
         nc.vector.reciprocal(inv_p_sum[:], p_sum[:])
         tp = wide("tp")
         tp_sum = column("tp_sum")
         nc.vector.scalar_tensor_tensor(tp[:], ta[:], 1.0, p[:], ALU.mult, ALU.mult, accum_out=tp_sum[:])
-        nc.gpsimd.tensor_scalar(r[:, :SLOTS], p[:], inv_p_sum[:], 0.0, ALU.mult, ALU.add)
+        nc.vector.tensor_scalar(r[:, :SLOTS], p[:], inv_p_sum[:], None, ALU.mult)
+        gout_mx = quantise("gout", round_rows("gout_bf", [gout_raw], nc.scalar.copy))
+        c = product("c", gout_mx, 0, listed_values, listed_value_scales[4:, :])
         mean = column("mean")
         nc.vector.tensor_scalar(mean[:], tp_sum[:], scalar_inv_p_sum[:], None, ALU.mult)
         nc.vector.scalar_tensor_tensor(tr[:, :SLOTS], ta[:], mean[:], r[:, :SLOTS], ALU.subtract, ALU.mult)
@@ -163,12 +168,6 @@ def tile_attend_hvdirect_agreed_s_kernel(
         nc.vector.tensor_tensor(rr[:], r[:].indirect(partner_list[:]), p[:], ALU.mult)
         half_inv_u = wide("half_inv_u")
         nc.scalar.activation(half_inv_u[:], rr[:], ACT.Abs_reciprocal_sqrt, bias=floor[:], scale=p_sum[:])
-
-        back_s = wide("back_s", tag="tp")
-        back_v = wide("back_v", tag="listed_keys")
-        placed = wide("placed", TOKENS, tag="value_words")
-        for window in (back_s, back_v, placed):
-            nc.gpsimd.memset(window[:], 0.0)
 
         own = wide("own")
         nc.vector.scalar_tensor_tensor(own[:], ta[:], mean[:], rr[:], ALU.subtract, ALU.mult)

@@ -14,19 +14,21 @@ ACT = mybir.ActivationFunctionType
 AXIS = mybir.AxisListType
 
 P = 128
-K = 512
+FEATURES = 512
 TOKENS = 2048
 SLOTS = 512
 ROWS = 128
 PACK = 4
-SPARE = 16
+QUADRANT = 32
 LIST_ROWS = 16
+SPARE = 16
+HALVES = (slice(0, SLOTS // 2), slice(SLOTS // 2, SLOTS))
 VECTOR_SHARE = 128
-SCALAR_SHARES = (384,)
 STORE_WIDTHS = (256, 512, 512, 512, 256)
 FLOOR = 2.0**-100
+GAIN = 128.0
 
-FLOPS = 3 * 2 * K * ROWS * SLOTS
+FLOPS = 3 * 2 * FEATURES * ROWS * SLOTS
 
 
 def tile_attend_hvdirect_agreed_s_kernel(
@@ -38,63 +40,70 @@ def tile_attend_hvdirect_agreed_s_kernel(
         sb = ctx.enter_context(tc.tile_pool(name="sb", bufs=1))
         psum = ctx.enter_context(tc.psum_pool(name="psum", bufs=1))
 
-        def wide(name, columns=SLOTS, tag=None):
-            return sb.tile([P, columns], F32, name=name, tag=tag or name, align_bytes=64)
+        def tile(name, shape, dtype, reuses=None):
+            return sb.tile(shape, dtype, name=name, tag=reuses or name, align_bytes=64)
 
-        def column(name, tag=None):
-            return sb.tile([P, 1], F32, name=name, tag=tag or name, align_bytes=64)
+        def wide(name, columns=SLOTS, reuses=None):
+            return tile(name, [P, columns], F32, reuses)
+
+        def column(name, reuses=None):
+            return tile(name, [P, 1], F32, reuses)
+
+        def entries(listed, slots):
+            return listed[:, slots.start // LIST_ROWS : slots.stop // LIST_ROWS]
 
         def load_words(name, words):
-            pool_words = sb.tile([P, TOKENS], I32, name=name, tag=name, align_bytes=64)
+            pool_words = tile(name, [P, TOKENS], I32)
             nc.sync.dma_start(out=pool_words[:], in_=words[0].rearrange("p n t -> p (n t)").bitcast(I32))
             return pool_words
 
         def load_scales(name, scales, first_row, queues):
-            pool_scales = sb.tile([P, TOKENS], U8, name=name, tag=name, align_bytes=64)
+            pool_scales = tile(name, [P, TOKENS], U8)
             nc.vector.memset(pool_scales[:].bitcast(I32), 0)
             for quadrant, queue in enumerate(queues):
+                top = QUADRANT * quadrant + first_row
                 queue.dma_start(
-                    out=pool_scales[32 * quadrant + first_row : 32 * quadrant + first_row + 4, :].bitcast(I32),
+                    out=pool_scales[top : top + 4, :].bitcast(I32),
                     in_=scales[0, 4 * quadrant : 4 * quadrant + 4, :].bitcast(I32),
                 )
             return pool_scales
 
         def load_rows(name, rows):
-            raw = sb.tile([P, PACK, ROWS], F32, name=name)
+            raw = tile(name, [P, PACK, ROWS], F32)
             nc.sync.dma_start(out=raw[:], in_=rows.rearrange("(p j) w -> p j w", j=PACK))
             return raw
 
         def gather_words(name, pool_words):
-            listed = sb.tile([P, SLOTS], U32, name=name, tag=name, align_bytes=64)
+            listed = tile(name, [P, SLOTS], U32)
             nc.vector.tensor_copy(listed[:], pool_words[:].bitcast(U32).indirect(token_list[:]))
             return listed
 
-        def gather_scales(name, pool_scales, tag):
-            listed = sb.tile([P, SLOTS], U8, name=name, tag=tag, align_bytes=64)
+        def gather_scales(name, pool_scales):
+            listed = tile(name, [P, SLOTS], U8)
             nc.vector.tensor_copy(listed[:], pool_scales[:].indirect(token_list[:]))
             return listed
 
         def round_rows(name, raws, copy):
-            grouped = sb.tile([P, len(raws) * ROWS, PACK], BF16, name=name, align_bytes=64)
+            grouped = tile(name, [P, len(raws), ROWS, PACK], BF16)
             for place, raw in enumerate(raws):
-                copy(out=grouped[:, place * ROWS : (place + 1) * ROWS, :], in_=raw[:].rearrange("p j w -> p w j"))
+                copy(out=grouped[:, place], in_=raw[:].rearrange("p j w -> p w j"))
             return grouped
 
         def quantise(name, grouped):
-            codes = sb.tile([P, grouped.shape[1]], U32, name=name + "_codes", align_bytes=64)
-            scales = sb.tile([P, grouped.shape[1]], U8, name=name + "_scales", align_bytes=64)
+            operands = grouped.shape[1]
+            codes = tile(name + "_codes", [P, operands * ROWS], U32)
+            scales = tile(name + "_scales", [P, operands * ROWS], U8)
             nc.vector.quantize_mx(
-                out=codes[:].bitcast(FP8X4), scales=scales[:], in_=grouped[:].rearrange("p w j -> p (w j)")
+                out=codes[:].bitcast(FP8X4), scales=scales[:], in_=grouped[:].rearrange("p o w j -> p (o w j)")
             )
-            return codes, scales
+            return [(codes[:, o * ROWS : (o + 1) * ROWS], scales[:, o * ROWS : (o + 1) * ROWS]) for o in range(operands)]
 
-        def product(name, rows_mx, place, listed_words, listed_scales):
-            rows = slice(place * ROWS, (place + 1) * ROWS)
+        def product(name, rows_mx, listed_words, listed_scales):
             bank = psum.tile([P, SLOTS], F32, name=name)
             nc.tensor.matmul_mx(
                 out=bank[:],
-                lhsT=rows_mx[0][:, rows].bitcast(FP8X4),
-                lhsT_scale=rows_mx[1][:, rows],
+                lhsT=rows_mx[0].bitcast(FP8X4),
+                lhsT_scale=rows_mx[1],
                 rhs=listed_words[:].bitcast(FP8X4),
                 rhs_scale=listed_scales,
                 start=True,
@@ -110,8 +119,8 @@ def tile_attend_hvdirect_agreed_s_kernel(
         key_words = load_words("key_words", keys_words)
         value_scales = load_scales("value_scales", vals_scales, 4, (nc.sync,) * 4)
         dquery_raw = load_rows("dquery_raw", dquery)
-        value_words = load_words("value_words", vals_words)
         gout_raw = load_rows("gout_raw", gout)
+        value_words = load_words("value_words", vals_words)
         nc.sync.dma_start(partner_list[:], offs4)
         res = column("res")
         nc.sync.dma_start(out=res[:], in_=reserve)
@@ -124,114 +133,126 @@ def tile_attend_hvdirect_agreed_s_kernel(
         nc.vector.memset(r[:, SLOTS:], 0.0)
         nc.vector.memset(tr[:, SLOTS:], 0.0)
         nc.vector.memset(floor[:], FLOOR)
-        back_s = wide("back_s")
-        back_v = wide("back_v")
+        moved_by_scalar = wide("moved_by_scalar")
+        moved_by_vector = wide("moved_by_vector")
         placed = wide("placed", TOKENS)
-        for window in (back_s, back_v, placed):
+        for window in (moved_by_scalar, moved_by_vector, placed):
             nc.vector.memset(window[:].bitcast(I32), 0)
 
-        listed_key_scales = gather_scales("listed_key_scales", key_scales, "listed_key_scales")
-        query_mx = quantise("query", round_rows("query_bf", [query_raw], nc.vector.tensor_copy))
+        listed_key_scales = gather_scales("listed_key_scales", key_scales)
+        (query_mx,) = quantise("query", round_rows("query_bf", [query_raw], nc.vector.tensor_copy))
         listed_keys = gather_words("listed_keys", key_words)
-        a = product("a", query_mx, 0, listed_keys, listed_key_scales[:])
-        listed_value_scales = gather_scales("listed_value_scales", value_scales, "listed_value_scales")
-        dquery_bf = round_rows("dquery_bf", [dquery_raw], nc.scalar.copy)
+        a = product("a", query_mx, listed_keys, listed_key_scales[:])
+        listed_value_scales = gather_scales("listed_value_scales", value_scales)
+        later_bf = round_rows("later_bf", [dquery_raw, gout_raw], nc.scalar.copy)
 
-        res2 = column("res2")
-        nc.vector.tensor_scalar(res2[:], res[:], 2.0, None, ALU.mult)
-        neg_max = column("neg_max", tag="value_scales")
+        neg_max = column("neg_max", reuses="dquery_raw")
         nc.vector.tensor_reduce(neg_max[:], a[:], AXIS.X, ALU.max, negate=True)
         p = wide("p")
         p_sum = column("p_sum")
         nc.scalar.activation(p[:], a[:], ACT.Exp, bias=neg_max[:], accum_out=p_sum[:])
+        root_inv_p_sum = column("root_inv_p_sum")
+        nc.scalar.activation(root_inv_p_sum[:], p_sum[:], ACT.Abs_reciprocal_sqrt, scale=p_sum[:])
 
-        scalar_inv_p_sum = column("scalar_inv_p_sum")
-        nc.scalar.activation(scalar_inv_p_sum[:], p_sum[:], ACT.Abs_reciprocal_sqrt, scale=p_sum[:])
-
-        ta = product("ta", quantise("dquery", dquery_bf), 0, listed_keys, listed_key_scales[:])
+        dquery_mx, gout_mx = quantise("later", later_bf)
+        ta = product("ta", dquery_mx, listed_keys, listed_key_scales[:])
         listed_values = gather_words("listed_values", value_words)
+        c = product("c", gout_mx, listed_values, listed_value_scales[4:, :])
 
-        inv_p_sum = column("inv_p_sum", tag="value_words")
+        inv_p_sum = column("inv_p_sum", reuses="value_words")
         nc.vector.reciprocal(inv_p_sum[:], p_sum[:])
         tp = wide("tp")
         tp_sum = column("tp_sum")
         nc.vector.scalar_tensor_tensor(tp[:], ta[:], 1.0, p[:], ALU.mult, ALU.mult, accum_out=tp_sum[:])
         nc.vector.tensor_scalar(r[:, :SLOTS], p[:], inv_p_sum[:], None, ALU.mult)
-        gout_mx = quantise("gout", round_rows("gout_bf", [gout_raw], nc.scalar.copy))
-        c = product("c", gout_mx, 0, listed_values, listed_value_scales[4:, :])
+        mean_for_tr = column("mean_for_tr")
+        nc.vector.tensor_scalar(mean_for_tr[:], tp_sum[:], inv_p_sum[:], None, ALU.mult)
         mean = column("mean")
-        nc.vector.tensor_scalar(mean[:], tp_sum[:], scalar_inv_p_sum[:], None, ALU.mult)
-        nc.vector.scalar_tensor_tensor(tr[:, :SLOTS], ta[:], mean[:], r[:, :SLOTS], ALU.subtract, ALU.mult)
+        nc.scalar.activation(mean[:], tp_sum[:], ACT.Copy, scale=root_inv_p_sum[:])
+        nc.vector.scalar_tensor_tensor(tr[:, :SLOTS], ta[:], mean_for_tr[:], r[:, :SLOTS], ALU.subtract, ALU.mult)
+
         tr_partner = wide("tr_partner")
         nc.scalar.activation(tr_partner[:], tr[:].indirect(partner_list[:]), ACT.Copy)
-        rr = wide("rr")
-        nc.vector.tensor_tensor(rr[:], r[:].indirect(partner_list[:]), p[:], ALU.mult)
-        half_inv_u = wide("half_inv_u")
-        nc.scalar.activation(half_inv_u[:], rr[:], ACT.Abs_reciprocal_sqrt, bias=floor[:], scale=p_sum[:])
-
-        own = wide("own")
-        nc.vector.scalar_tensor_tensor(own[:], ta[:], mean[:], rr[:], ALU.subtract, ALU.mult)
-        other = wide("other")
-        nc.vector.tensor_tensor(other[:], tr_partner[:], p[:], ALU.mult)
+        pair = wide("pair", reuses="mean_for_tr")
+        for half in HALVES:
+            nc.vector.tensor_tensor(pair[:, half], r[:].indirect(entries(partner_list, half)), p[:, half], ALU.mult)
+        inv_pu = wide("inv_pu")
+        nc.scalar.activation(inv_pu[:], pair[:], ACT.Abs_reciprocal_sqrt, bias=floor[:], scale=p_sum[:])
+        own_move = wide("own_move")
+        for half in HALVES:
+            nc.vector.scalar_tensor_tensor(own_move[:, half], ta[:, half], mean[:], pair[:, half], ALU.subtract, ALU.mult)
+        partner_move = wide("partner_move")
+        nc.vector.tensor_tensor(partner_move[:], tr_partner[:], p[:], ALU.mult)
         u = wide("u")
         u_sum = column("u_sum")
-        nc.vector.scalar_tensor_tensor(u[:], rr[:], 1.0, half_inv_u[:], ALU.mult, ALU.mult, accum_out=u_sum[:])
-        trr = wide("trr")
-        nc.vector.tensor_tensor(trr[:], own[:], other[:], ALU.add)
-        z_256th = column("z_256th")
-        nc.vector.tensor_scalar(z_256th[:], u_sum[:], res[:], 1.0 / 128.0, ALU.add, ALU.mult)
+        nc.vector.scalar_tensor_tensor(u[:], pair[:], 1.0, inv_pu[:], ALU.mult, ALU.mult, accum_out=u_sum[:])
+
+        pair_move = wide("pair_move")
+        first, second = HALVES
+        nc.vector.tensor_tensor(pair_move[:, first], own_move[:, first], partner_move[:, first], ALU.add)
+        z_over_gain = column("z_over_gain")
+        nc.vector.tensor_scalar(z_over_gain[:], u_sum[:], res[:], 1.0 / GAIN, ALU.add, ALU.mult)
+        nc.vector.tensor_tensor(pair_move[:, second], own_move[:, second], partner_move[:, second], ALU.add)
+        gain_over_z = column("gain_over_z")
+        nc.vector.reciprocal(gain_over_z[:], z_over_gain[:])
         cu = wide("cu")
         cu_sum = column("cu_sum")
         nc.vector.scalar_tensor_tensor(cu[:], c[:], 1.0, u[:], ALU.mult, ALU.mult, accum_out=cu_sum[:])
-        inv_z_256 = column("inv_z_256")
-        nc.vector.reciprocal(inv_z_256[:], z_256th[:])
         neg_inv_z = column("neg_inv_z")
-        nc.vector.tensor_scalar(neg_inv_z[:], inv_z_256[:], -1.0 / 128.0, None, ALU.mult)
-        tu = wide("tu")
-        tu_sum = column("tu_sum")
+        nc.vector.tensor_scalar(neg_inv_z[:], gain_over_z[:], -1.0 / GAIN, None, ALU.mult)
+        scaled_tu = wide("scaled_tu")
+        scaled_tu_sum = column("scaled_tu_sum")
         nc.vector.scalar_tensor_tensor(
-            tu[:], trr[:], inv_z_256[:], half_inv_u[:], ALU.mult, ALU.mult, accum_out=tu_sum[:]
+            scaled_tu[:], pair_move[:], gain_over_z[:], inv_pu[:], ALU.mult, ALU.mult, accum_out=scaled_tu_sum[:]
         )
         neg_gamma = column("neg_gamma")
         nc.vector.tensor_scalar(neg_gamma[:], cu_sum[:], neg_inv_z[:], None, ALU.mult)
-        neg_kappa = column("neg_kappa")
-        nc.vector.tensor_scalar(neg_kappa[:], tu_sum[:], neg_inv_z[:], None, ALU.mult)
-        res_z = column("res_z")
-        nc.scalar.activation(res_z[:], res2[:], ACT.Copy, scale=inv_z_256[:])
-        neg_half_d = column("neg_half_d")
-        nc.scalar.activation(neg_half_d[:], neg_gamma[:], ACT.Copy, scale=res_z[:])
+
+        res_factor = column("res_factor")
+        nc.scalar.activation(res_factor[:], res[:], ACT.Copy, scale=gain_over_z[:])
+        twice_res_factor = column("twice_res_factor")
+        nc.scalar.activation(twice_res_factor[:], res_factor[:], ACT.Copy, scale=2.0)
+        tr_factor = column("tr_factor")
+        nc.scalar.activation(tr_factor[:], neg_gamma[:], ACT.Copy, scale=twice_res_factor[:])
         tr_term = wide("tr_term")
-        nc.scalar.activation(tr_term[:], tr[:, :SLOTS], ACT.Copy, scale=neg_half_d[:])
+        nc.scalar.activation(tr_term[:], tr[:, :SLOTS], ACT.Copy, scale=tr_factor[:])
+
+        cu_factor = column("cu_factor")
+        nc.vector.tensor_scalar(cu_factor[:], scaled_tu_sum[:], neg_inv_z[:], None, ALU.mult)
         ctu = wide("ctu")
         ctu_sum = column("ctu_sum")
-        nc.vector.scalar_tensor_tensor(ctu[:], c[:], neg_gamma[:], tu[:], ALU.add, ALU.mult, accum_out=ctu_sum[:])
-        kappa_gamma = column("kappa_gamma")
-        nc.vector.tensor_scalar(kappa_gamma[:], neg_kappa[:], neg_gamma[:], None, ALU.mult)
-        neg_beta = column("neg_beta")
-        nc.vector.tensor_scalar(neg_beta[:], ctu_sum[:], neg_inv_z[:], kappa_gamma[:], ALU.mult, ALU.add)
+        nc.vector.scalar_tensor_tensor(
+            ctu[:], c[:], neg_gamma[:], scaled_tu[:], ALU.add, ALU.mult, accum_out=ctu_sum[:]
+        )
+        gamma_part = column("gamma_part")
+        nc.vector.tensor_scalar(gamma_part[:], cu_factor[:], neg_gamma[:], None, ALU.mult)
+        c_terms_sum = column("c_terms_sum")
+        nc.vector.tensor_scalar(c_terms_sum[:], cu_sum[:], cu_factor[:], ctu_sum[:], ALU.mult, ALU.add)
+        u_factor = column("u_factor")
+        nc.vector.tensor_scalar(u_factor[:], ctu_sum[:], neg_inv_z[:], gamma_part[:], ALU.mult, ALU.add)
         c_terms = wide("c_terms")
-        nc.vector.scalar_tensor_tensor(c_terms[:], cu[:], neg_kappa[:], ctu[:], ALU.mult, ALU.add)
-        g = wide("g")
+        nc.vector.scalar_tensor_tensor(c_terms[:], cu[:], cu_factor[:], ctu[:], ALU.mult, ALU.add)
         g_sum = column("g_sum")
-        nc.vector.scalar_tensor_tensor(g[:], u[:], neg_beta[:], c_terms[:], ALU.mult, ALU.add, accum_out=g_sum[:])
+        nc.vector.tensor_scalar(g_sum[:], u_sum[:], u_factor[:], c_terms_sum[:], ALU.mult, ALU.add)
+        g = wide("g")
+        nc.vector.scalar_tensor_tensor(g[:], u[:], u_factor[:], c_terms[:], ALU.mult, ALU.add)
 
-        first_slot = VECTOR_SHARE
-        for share in SCALAR_SHARES:
-            entries = partner_list[:, first_slot // LIST_ROWS : (first_slot + share) // LIST_ROWS]
-            nc.scalar.activation(back_s[:].indirect(entries), g[:, first_slot : first_slot + share], ACT.Copy)
-            first_slot += share
-        nc.vector.tensor_copy(back_v[:].indirect(partner_list[:, : VECTOR_SHARE // LIST_ROWS]), g[:, :VECTOR_SHARE])
+        by_vector, by_scalar = slice(0, VECTOR_SHARE), slice(VECTOR_SHARE, SLOTS)
+        nc.scalar.activation(moved_by_scalar[:].indirect(entries(partner_list, by_scalar)), g[:, by_scalar], ACT.Copy)
         softmax_term = wide("softmax_term")
         nc.vector.scalar_tensor_tensor(softmax_term[:], r[:, :SLOTS], g_sum[:], tr_term[:], ALU.mult, ALU.subtract)
-        both = wide("both")
-        nc.vector.tensor_tensor(both[:], g[:], back_v[:], ALU.add)
+        nc.vector.tensor_copy(moved_by_vector[:].indirect(entries(partner_list, by_vector)), g[:, by_vector])
+        staying = wide("staying")
+        for half in HALVES:
+            nc.vector.scalar_tensor_tensor(staying[:, half], softmax_term[:, half], -2.0, g[:, half], ALU.mult, ALU.add)
         partial = wide("partial")
-        nc.vector.scalar_tensor_tensor(partial[:], softmax_term[:], -2.0, both[:], ALU.mult, ALU.add)
-        nc.vector.tensor_tensor(placed[:].indirect(token_list[:]), partial[:], back_s[:], ALU.add)
+        for half in HALVES:
+            nc.vector.tensor_tensor(partial[:, half], staying[:, half], moved_by_vector[:, half], ALU.add)
 
-        first = 0
+        nc.vector.tensor_tensor(placed[:].indirect(token_list[:]), partial[:], moved_by_scalar[:], ALU.add)
+        start = 0
         for width in STORE_WIDTHS:
-            cols = slice(first, first + width)
+            cols = slice(start, start + width)
             nc.vector.tensor_tensor(result[:, cols], result[:, cols], placed[:, cols], ALU.add)
             nc.sync.dma_start(out=out[:, cols], in_=result[:, cols])
-            first += width
+            start += width

@@ -20,6 +20,7 @@ SLOTS = 512
 ROWS = 128
 PACK = 4
 QUADRANT = 32
+SCALE_ROWS = 4
 LIST_ROWS = 16
 SPARE = 16
 HALVES = (slice(0, SLOTS // 2), slice(SLOTS // 2, SLOTS))
@@ -49,8 +50,8 @@ def tile_attend_hvdirect_agreed_s_kernel(
         def column(name, reuses=None):
             return tile(name, [P, 1], F32, reuses)
 
-        def entries(listed, slots):
-            return listed[:, slots.start // LIST_ROWS : slots.stop // LIST_ROWS]
+        def entries(offsets, slots):
+            return offsets[:, slots.start // LIST_ROWS : slots.stop // LIST_ROWS]
 
         def load_words(name, words):
             pool_words = tile(name, [P, TOKENS], I32)
@@ -63,8 +64,8 @@ def tile_attend_hvdirect_agreed_s_kernel(
             for quadrant, queue in enumerate(queues):
                 top = QUADRANT * quadrant + first_row
                 queue.dma_start(
-                    out=pool_scales[top : top + 4, :].bitcast(I32),
-                    in_=scales[0, 4 * quadrant : 4 * quadrant + 4, :].bitcast(I32),
+                    out=pool_scales[top : top + SCALE_ROWS, :].bitcast(I32),
+                    in_=scales[0, SCALE_ROWS * quadrant : SCALE_ROWS * (quadrant + 1), :].bitcast(I32),
                 )
             return pool_scales
 
@@ -117,7 +118,7 @@ def tile_attend_hvdirect_agreed_s_kernel(
         query_raw = load_rows("query_raw", query)
         key_scales = load_scales("key_scales", keys_scales, 0, (nc.sync, nc.sync, nc.scalar, nc.scalar))
         key_words = load_words("key_words", keys_words)
-        value_scales = load_scales("value_scales", vals_scales, 4, (nc.sync,) * 4)
+        value_scales = load_scales("value_scales", vals_scales, SCALE_ROWS, (nc.sync,) * 4)
         dquery_raw = load_rows("dquery_raw", dquery)
         gout_raw = load_rows("gout_raw", gout)
         value_words = load_words("value_words", vals_words)
@@ -157,9 +158,9 @@ def tile_attend_hvdirect_agreed_s_kernel(
         dquery_mx, gout_mx = quantise("later", later_bf)
         ta = product("ta", dquery_mx, listed_keys, listed_key_scales[:])
         listed_values = gather_words("listed_values", value_words)
-        c = product("c", gout_mx, listed_values, listed_value_scales[4:, :])
+        c = product("c", gout_mx, listed_values, listed_value_scales[SCALE_ROWS:, :])
 
-        inv_p_sum = column("inv_p_sum", reuses="value_words")
+        inv_p_sum = column("inv_p_sum")
         nc.vector.reciprocal(inv_p_sum[:], p_sum[:])
         tp = wide("tp")
         tp_sum = column("tp_sum")
@@ -167,15 +168,16 @@ def tile_attend_hvdirect_agreed_s_kernel(
         nc.vector.tensor_scalar(r[:, :SLOTS], p[:], inv_p_sum[:], None, ALU.mult)
         mean_for_tr = column("mean_for_tr")
         nc.vector.tensor_scalar(mean_for_tr[:], tp_sum[:], inv_p_sum[:], None, ALU.mult)
-        mean = column("mean")
-        nc.scalar.activation(mean[:], tp_sum[:], ACT.Copy, scale=root_inv_p_sum[:])
         nc.vector.scalar_tensor_tensor(tr[:, :SLOTS], ta[:], mean_for_tr[:], r[:, :SLOTS], ALU.subtract, ALU.mult)
 
         tr_partner = wide("tr_partner")
         nc.scalar.activation(tr_partner[:], tr[:].indirect(partner_list[:]), ACT.Copy)
         pair = wide("pair", reuses="mean_for_tr")
-        for half in HALVES:
-            nc.vector.tensor_tensor(pair[:, half], r[:].indirect(entries(partner_list, half)), p[:, half], ALU.mult)
+        first, second = HALVES
+        nc.vector.tensor_tensor(pair[:, first], r[:].indirect(entries(partner_list, first)), p[:, first], ALU.mult)
+        mean = column("mean", reuses="inv_p_sum")
+        nc.vector.tensor_scalar(mean[:], tp_sum[:], root_inv_p_sum[:], None, ALU.mult)
+        nc.vector.tensor_tensor(pair[:, second], r[:].indirect(entries(partner_list, second)), p[:, second], ALU.mult)
         inv_pu = wide("inv_pu")
         nc.scalar.activation(inv_pu[:], pair[:], ACT.Abs_reciprocal_sqrt, bias=floor[:], scale=p_sum[:])
         own_move = wide("own_move")
@@ -188,7 +190,6 @@ def tile_attend_hvdirect_agreed_s_kernel(
         nc.vector.scalar_tensor_tensor(u[:], pair[:], 1.0, inv_pu[:], ALU.mult, ALU.mult, accum_out=u_sum[:])
 
         pair_move = wide("pair_move")
-        first, second = HALVES
         nc.vector.tensor_tensor(pair_move[:, first], own_move[:, first], partner_move[:, first], ALU.add)
         z_over_gain = column("z_over_gain")
         nc.vector.tensor_scalar(z_over_gain[:], u_sum[:], res[:], 1.0 / GAIN, ALU.add, ALU.mult)

from contextlib import ExitStack

import concourse.mybir as mybir

F32 = mybir.dt.float32
BF16 = mybir.dt.bfloat16
I32 = mybir.dt.int32
U32 = mybir.dt.uint32
U16 = mybir.dt.uint16
U8 = mybir.dt.uint8
FP8X4 = mybir.dt.float8_e4m3fn_x4
ALU = mybir.AluOpType
ACT = mybir.ActivationFunctionType
AXIS = mybir.AxisListType

P = 128
FEATURES = 512
TOKENS = 2048
SLOTS = 512
ROWS = 128
PACK = 4
QUADRANT = 32
SCALE_ROWS = 4
LIST_ROWS = 16
SPARE = 16
HALVES = (slice(0, SLOTS // 2), slice(SLOTS // 2, SLOTS))
VECTOR_SHARE = 128
STORE_WIDTHS = (256, 512, 512, 512, 256)
FLOOR = 2.0**-100
GAIN = 128.0

FLOPS = 3 * 2 * FEATURES * ROWS * SLOTS


def tile_attend_hvdirect_agreed_s_kernel(
    tc, query, keys_words, keys_scales, reserve, gout, vals_words, vals_scales, dquery, base, offs4, offs, out
):
    nc = tc.nc
    with ExitStack() as ctx:
        lists = ctx.enter_context(tc.tile_pool(name="lists", bufs=1))
        sb = ctx.enter_context(tc.tile_pool(name="sb", bufs=1))
        psum = ctx.enter_context(tc.psum_pool(name="psum", bufs=1))

        def tile(name, shape, dtype, reuses=None):
            return sb.tile(shape, dtype, name=name, tag=reuses or name, align_bytes=64)

        def wide(name, columns=SLOTS, reuses=None):
            return tile(name, [P, columns], F32, reuses)

        def column(name, reuses=None):
            return tile(name, [P, 1], F32, reuses)

        def entries(offsets, slots):
            return offsets[:, slots.start // LIST_ROWS : slots.stop // LIST_ROWS]

        def load_words(name, words):
            pool_words = tile(name, [P, TOKENS], I32)
            nc.sync.dma_start(out=pool_words[:], in_=words[0].rearrange("p n t -> p (n t)").bitcast(I32))
            return pool_words

        def load_scales(name, scales, first_row, queues):
            pool_scales = tile(name, [P, TOKENS], U8)
            nc.vector.memset(pool_scales[:].bitcast(I32), 0)
            for quadrant, queue in enumerate(queues):
                top = QUADRANT * quadrant + first_row
                queue.dma_start(
                    out=pool_scales[top : top + SCALE_ROWS, :].bitcast(I32),
                    in_=scales[0, SCALE_ROWS * quadrant : SCALE_ROWS * (quadrant + 1), :].bitcast(I32),
                )
            return pool_scales

        def load_rows(name, rows):
            raw = tile(name, [P, PACK, ROWS], F32)
            nc.sync.dma_start(out=raw[:], in_=rows.rearrange("(p j) w -> p j w", j=PACK))
            return raw

        def gather_words(name, pool_words):
            listed = tile(name, [P, SLOTS], U32)
            nc.vector.tensor_copy(listed[:], pool_words[:].bitcast(U32).indirect(token_list[:]))
            return listed

        def gather_scales(name, pool_scales):
            listed = tile(name, [P, SLOTS], U8)
            nc.vector.tensor_copy(listed[:], pool_scales[:].indirect(token_list[:]))
            return listed

        def round_rows(name, raws, copy):
            grouped = tile(name, [P, len(raws), ROWS, PACK], BF16)
            for place, raw in enumerate(raws):
                copy(out=grouped[:, place], in_=raw[:].rearrange("p j w -> p w j"))
            return grouped

        def quantise(name, grouped):
            operands = grouped.shape[1]
            codes = tile(name + "_codes", [P, operands * ROWS], U32)
            scales = tile(name + "_scales", [P, operands * ROWS], U8)
            nc.vector.quantize_mx(
                out=codes[:].bitcast(FP8X4), scales=scales[:], in_=grouped[:].rearrange("p o w j -> p (o w j)")
            )
            return [(codes[:, o * ROWS : (o + 1) * ROWS], scales[:, o * ROWS : (o + 1) * ROWS]) for o in range(operands)]

        def product(name, rows_mx, listed_words, listed_scales):
            bank = psum.tile([P, SLOTS], F32, name=name)
            nc.tensor.matmul_mx(
                out=bank[:],
                lhsT=rows_mx[0].bitcast(FP8X4),
                lhsT_scale=rows_mx[1],
                rhs=listed_words[:].bitcast(FP8X4),
                rhs_scale=listed_scales,
                start=True,
                stop=True,
            )
            return bank

        token_list = lists.tile([P, SLOTS // LIST_ROWS], U16, name="token_list")
        partner_list = lists.tile([P, SLOTS // LIST_ROWS], U16, name="partner_list")
        nc.sync.dma_start(token_list[:], offs)
        query_raw = load_rows("query_raw", query)
        key_scales = load_scales("key_scales", keys_scales, 0, (nc.sync, nc.sync, nc.scalar, nc.scalar))
        key_words = load_words("key_words", keys_words)
        value_scales = load_scales("value_scales", vals_scales, SCALE_ROWS, (nc.sync,) * 4)
        dquery_raw = load_rows("dquery_raw", dquery)
        gout_raw = load_rows("gout_raw", gout)
        value_words = load_words("value_words", vals_words)
        nc.sync.dma_start(partner_list[:], offs4)
        res = column("res")
        nc.sync.dma_start(out=res[:], in_=reserve)
        result = wide("result", TOKENS)
        nc.sync.dma_start(out=result[:], in_=base)

        r = wide("r", SLOTS + SPARE)
        tr = wide("tr", SLOTS + SPARE)
        floor = column("floor")
        nc.vector.memset(r[:, SLOTS:], 0.0)
        nc.vector.memset(tr[:, SLOTS:], 0.0)
        nc.vector.memset(floor[:], FLOOR)
        moved_by_scalar = wide("moved_by_scalar")
        moved_by_vector = wide("moved_by_vector")
        placed = wide("placed", TOKENS)
        for window in (moved_by_scalar, moved_by_vector, placed):
            nc.vector.memset(window[:].bitcast(I32), 0)

        listed_key_scales = gather_scales("listed_key_scales", key_scales)
        (query_mx,) = quantise("query", round_rows("query_bf", [query_raw], nc.vector.tensor_copy))
        listed_keys = gather_words("listed_keys", key_words)
        a = product("a", query_mx, listed_keys, listed_key_scales[:])
        listed_value_scales = gather_scales("listed_value_scales", value_scales)
        later_bf = round_rows("later_bf", [dquery_raw, gout_raw], nc.scalar.copy)

        neg_max = column("neg_max", reuses="dquery_raw")
        nc.vector.tensor_reduce(neg_max[:], a[:], AXIS.X, ALU.max, negate=True)
        p = wide("p")
        p_sum = column("p_sum")
        nc.scalar.activation(p[:], a[:], ACT.Exp, bias=neg_max[:], accum_out=p_sum[:])
        root_inv_p_sum = column("root_inv_p_sum")
        nc.scalar.activation(root_inv_p_sum[:], p_sum[:], ACT.Abs_reciprocal_sqrt, scale=p_sum[:])

        dquery_mx, gout_mx = quantise("later", later_bf)
        ta = product("ta", dquery_mx, listed_keys, listed_key_scales[:])
        listed_values = gather_words("listed_values", value_words)
        c = product("c", gout_mx, listed_values, listed_value_scales[SCALE_ROWS:, :])

        inv_p_sum = column("inv_p_sum")
        nc.vector.reciprocal(inv_p_sum[:], p_sum[:])
        tp = wide("tp")
        tp_sum = column("tp_sum")
        nc.vector.scalar_tensor_tensor(tp[:], ta[:], 1.0, p[:], ALU.mult, ALU.mult, accum_out=tp_sum[:])
        nc.vector.tensor_scalar(r[:, :SLOTS], p[:], inv_p_sum[:], None, ALU.mult)
        mean_for_tr = column("mean_for_tr")
        nc.vector.tensor_scalar(mean_for_tr[:], tp_sum[:], inv_p_sum[:], None, ALU.mult)
        nc.vector.scalar_tensor_tensor(tr[:, :SLOTS], ta[:], mean_for_tr[:], r[:, :SLOTS], ALU.subtract, ALU.mult)

        tr_partner = wide("tr_partner")
        nc.scalar.activation(tr_partner[:], tr[:].indirect(partner_list[:]), ACT.Copy)
        pair = wide("pair", reuses="mean_for_tr")
        first, second = HALVES
        nc.vector.tensor_tensor(pair[:, first], r[:].indirect(entries(partner_list, first)), p[:, first], ALU.mult)
        mean = column("mean", reuses="inv_p_sum")
        nc.vector.tensor_scalar(mean[:], tp_sum[:], root_inv_p_sum[:], None, ALU.mult)
        nc.vector.tensor_tensor(pair[:, second], r[:].indirect(entries(partner_list, second)), p[:, second], ALU.mult)
        inv_pu = wide("inv_pu")
        nc.scalar.activation(inv_pu[:], pair[:], ACT.Abs_reciprocal_sqrt, bias=floor[:], scale=p_sum[:])
        own_move = wide("own_move")
        for half in HALVES:
            nc.vector.scalar_tensor_tensor(own_move[:, half], ta[:, half], mean[:], pair[:, half], ALU.subtract, ALU.mult)
        partner_move = wide("partner_move")
        nc.vector.tensor_tensor(partner_move[:], tr_partner[:], p[:], ALU.mult)
        u = wide("u")
        u_sum = column("u_sum")
        nc.vector.scalar_tensor_tensor(u[:], pair[:], 1.0, inv_pu[:], ALU.mult, ALU.mult, accum_out=u_sum[:])

        pair_move = wide("pair_move")
        nc.vector.tensor_tensor(pair_move[:, first], own_move[:, first], partner_move[:, first], ALU.add)
        z_over_gain = column("z_over_gain")
        nc.vector.tensor_scalar(z_over_gain[:], u_sum[:], res[:], 1.0 / GAIN, ALU.add, ALU.mult)
        nc.vector.tensor_tensor(pair_move[:, second], own_move[:, second], partner_move[:, second], ALU.add)
        gain_over_z = column("gain_over_z")
        nc.vector.reciprocal(gain_over_z[:], z_over_gain[:])
        cu = wide("cu")
        cu_sum = column("cu_sum")
        nc.vector.scalar_tensor_tensor(cu[:], c[:], 1.0, u[:], ALU.mult, ALU.mult, accum_out=cu_sum[:])
        neg_inv_z = column("neg_inv_z")
        nc.vector.tensor_scalar(neg_inv_z[:], gain_over_z[:], -1.0 / GAIN, None, ALU.mult)
        scaled_tu = wide("scaled_tu")
        scaled_tu_sum = column("scaled_tu_sum")
        nc.vector.scalar_tensor_tensor(
            scaled_tu[:], pair_move[:], gain_over_z[:], inv_pu[:], ALU.mult, ALU.mult, accum_out=scaled_tu_sum[:]
        )
        neg_gamma = column("neg_gamma")
        nc.vector.tensor_scalar(neg_gamma[:], cu_sum[:], neg_inv_z[:], None, ALU.mult)

        res_factor = column("res_factor")
        nc.scalar.activation(res_factor[:], res[:], ACT.Copy, scale=gain_over_z[:])
        twice_res_factor = column("twice_res_factor")
        nc.scalar.activation(twice_res_factor[:], res_factor[:], ACT.Copy, scale=2.0)
        tr_factor = column("tr_factor")
        nc.scalar.activation(tr_factor[:], neg_gamma[:], ACT.Copy, scale=twice_res_factor[:])
        tr_term = wide("tr_term")
        nc.scalar.activation(tr_term[:], tr[:, :SLOTS], ACT.Copy, scale=tr_factor[:])

        cu_factor = column("cu_factor")
        nc.vector.tensor_scalar(cu_factor[:], scaled_tu_sum[:], neg_inv_z[:], None, ALU.mult)
        ctu = wide("ctu")
        ctu_sum = column("ctu_sum")
        nc.vector.scalar_tensor_tensor(
            ctu[:], c[:], neg_gamma[:], scaled_tu[:], ALU.add, ALU.mult, accum_out=ctu_sum[:]
        )
        gamma_part = column("gamma_part")
        nc.vector.tensor_scalar(gamma_part[:], cu_factor[:], neg_gamma[:], None, ALU.mult)
        c_terms_sum = column("c_terms_sum")
        nc.vector.tensor_scalar(c_terms_sum[:], cu_sum[:], cu_factor[:], ctu_sum[:], ALU.mult, ALU.add)
        u_factor = column("u_factor")
        nc.vector.tensor_scalar(u_factor[:], ctu_sum[:], neg_inv_z[:], gamma_part[:], ALU.mult, ALU.add)
        c_terms = wide("c_terms")
        nc.vector.scalar_tensor_tensor(c_terms[:], cu[:], cu_factor[:], ctu[:], ALU.mult, ALU.add)
        g_sum = column("g_sum")
        nc.vector.tensor_scalar(g_sum[:], u_sum[:], u_factor[:], c_terms_sum[:], ALU.mult, ALU.add)
        g = wide("g")
        nc.vector.scalar_tensor_tensor(g[:], u[:], u_factor[:], c_terms[:], ALU.mult, ALU.add)

        by_vector, by_scalar = slice(0, VECTOR_SHARE), slice(VECTOR_SHARE, SLOTS)
        nc.scalar.activation(moved_by_scalar[:].indirect(entries(partner_list, by_scalar)), g[:, by_scalar], ACT.Copy)
        softmax_term = wide("softmax_term")
        nc.vector.scalar_tensor_tensor(softmax_term[:], r[:, :SLOTS], g_sum[:], tr_term[:], ALU.mult, ALU.subtract)
        nc.vector.tensor_copy(moved_by_vector[:].indirect(entries(partner_list, by_vector)), g[:, by_vector])
        staying = wide("staying")
        for half in HALVES:
            nc.vector.scalar_tensor_tensor(staying[:, half], softmax_term[:, half], -2.0, g[:, half], ALU.mult, ALU.add)
        partial = wide("partial")
        for half in HALVES:
            nc.vector.tensor_tensor(partial[:, half], staying[:, half], moved_by_vector[:, half], ALU.add)

        nc.vector.tensor_tensor(placed[:].indirect(token_list[:]), partial[:], moved_by_scalar[:], ALU.add)
        start = 0
        for width in STORE_WIDTHS:
            cols = slice(start, start + width)
            nc.vector.tensor_tensor(result[:, cols], result[:, cols], placed[:, cols], ALU.add)
            nc.sync.dma_start(out=out[:, cols], in_=result[:, cols])
            start += width
